import numpy as np
import ml_dtypes


def mxq(x, axis, fmt="e4m3"):
    dtype, down = {"e4m3": (ml_dtypes.float8_e4m3fn, 7), "e5m2": (ml_dtypes.float8_e5m2, 14)}[fmt]
    v = np.moveaxis(np.asarray(x, np.float32).astype(ml_dtypes.bfloat16).astype(np.float64), axis, -1)
    blocks = v.reshape(v.shape[:-1] + (-1, 32))
    amax = np.abs(blocks).max(-1, keepdims=True)
    byte = np.maximum(np.where(amax > 0, np.frexp(amax)[1] - 1 + 127, 0) - down, 1)
    scale = np.exp2(byte - 127.0)
    codes = (blocks / scale).astype(np.float32).astype(dtype).astype(np.float64)
    return np.moveaxis((codes * scale).reshape(v.shape), -1, axis)


WIDE = False


def mx_kscale(k):
    if not WIDE:
        return np.ones(k)
    levels = np.array([10, -10, 5, -5, 0])
    if k % 512:
        return np.exp2(np.random.permutation(np.resize(levels, k // 32))).repeat(32)
    a = np.empty((k // 512, 16))
    for p in range(k // 512):
        a[p, :8] = np.random.permutation(np.resize(levels, 8))
        for g in range(8):
            far = levels[np.abs(levels - a[p, g]) >= 10]
            a[p, g + 8] = far[np.random.randint(len(far))]
    return np.exp2(a.ravel()).repeat(32)


def f64(x):
    return np.asarray(x).astype(np.float64)


def striped(idx):
    return np.tile(idx.reshape(-1, 16).T, (8, 1)).astype(np.uint16)


def unstriped(offs):
    return offs[:16].T.reshape(-1).astype(np.int64)


E2M1 = np.array([0.0, 0.5, 1.0, 1.5, 2.0, 3.0, 4.0, 6.0, -0.0, -0.5, -1.0, -1.5, -2.0, -3.0, -4.0, -6.0])


def pack_weight(w, fmt):
    k, n = w.shape
    w = f64(np.asarray(w, np.float32).astype(ml_dtypes.bfloat16)).reshape(k // 32, 32, n)
    amax = np.abs(w).max(1)
    if fmt == "e4m3":
        byte = np.frexp(amax)[1] - 1 + 127 - 7
    else:
        mant, ex = np.frexp(amax / 6.0)
        byte = np.where(mant > 0.5, ex, ex - 1) + 127
    byte = np.clip(np.where(amax > 0, byte, 1), 1, 254)
    scaled = (w * np.exp2(127.0 - byte)[:, None, :]).reshape(k, n).astype(np.float32)
    by_word = np.ascontiguousarray(scaled.reshape(k // 512, 128, 4, n).transpose(0, 1, 3, 2))
    if fmt == "e4m3":
        words = by_word.astype(ml_dtypes.float8_e4m3fn).view(np.uint8)
    else:
        c = by_word.astype(ml_dtypes.float4_e2m1fn).view(np.uint8) & 0xF
        words = (c[..., 0::2] | (c[..., 1::2] << 4)).reshape(k // 512, 128, 2 * n)
    return np.ascontiguousarray(words), np.ascontiguousarray(byte.astype(np.uint8).reshape(k // 512, 16, n))


def unpack_weight(words, scales, fmt):
    g, _, n = scales.shape
    words = np.ascontiguousarray(words).reshape(g, 128, n, -1)
    if fmt == "e4m3":
        vals = words.view(ml_dtypes.float8_e4m3fn).astype(np.float64)
    else:
        nib = np.empty((g, 128, n, 4), np.uint8)
        nib[..., 0::2] = words & 0xF
        nib[..., 1::2] = words >> 4
        vals = E2M1[nib]
    vals = vals * np.repeat(np.exp2(scales.astype(np.float64) - 127.0), 8, axis=1)[..., None]
    return vals.transpose(0, 1, 3, 2).reshape(g * 512, n)


def sigmoid(v):
    return 1.0 / (1.0 + np.exp(-np.maximum(v, -700.0)))


K, T, Q, E, C, D, H = 1024, 768, 512, 2, 256, 256, 512
N = 128


def by_expert(wq, xq, C):
    return np.concatenate([wq[e].T @ xq[:, e * C:(e + 1) * C] for e in range(E)], axis=1)


def setup_inputs():
    n = np.random.standard_normal
    s = mx_kscale(K)
    u = mx_kscale(H)
    slot_token = np.random.permutation(T)[:E * C]
    slots2 = np.concatenate([np.random.permutation(Q)[:D] for e in range(E)])
    x = pack_weight(n((K, Q)) * s[:, None], "e4m3")
    w1 = [pack_weight(m, "e4m3") for m in n((E, K, H)) / np.sqrt(K) / s[None, :, None]]
    w3 = [pack_weight(m, "e4m3") for m in n((E, K, H)) / np.sqrt(K) / s[None, :, None] * u]
    w2 = [pack_weight(m, "e4m3") for m in n((E, H, N)) / np.sqrt(H) / u[None, :, None]]
    return {
        "x_words": x[0],
        "x_scales": x[1],
        "xo": (n((K, T)) * s[:, None]).astype(np.float32),
        "w1_words": np.stack([m[0] for m in w1]),
        "w1_scales": np.stack([m[1] for m in w1]),
        "w3_words": np.stack([m[0] for m in w3]),
        "w3_scales": np.stack([m[1] for m in w3]),
        "w2_words": np.stack([m[0] for m in w2]),
        "w2_scales": np.stack([m[1] for m in w2]),
        "gate": np.tile(np.random.uniform(0.2, 1.0, E * C), (128, 1)).astype(np.float32),
        "offs": striped(slot_token),
        "offs2": striped(slots2),
    }


def reference(x_words, x_scales, xo, w1_words, w1_scales, w3_words, w3_scales, w2_words, w2_scales, gate, offs, offs2):
    w1 = np.stack([unpack_weight(w1_words[e], w1_scales[e], "e4m3") for e in range(E)])
    w3 = np.stack([unpack_weight(w3_words[e], w3_scales[e], "e4m3") for e in range(E)])
    w2 = np.stack([unpack_weight(w2_words[e], w2_scales[e], "e4m3") for e in range(E)])
    idx, idx2 = unstriped(offs), unstriped(offs2)
    xq = mxq(f64(xo)[:, idx], 0, "e4m3")
    rq = unpack_weight(x_words, x_scales, "e4m3")[:, idx2]
    h = sigmoid(by_expert(w1, xq, C)) * by_expert(w3, xq, C)
    y = by_expert(w2, mxq(h, 0, "e4m3"), C)
    h = sigmoid(by_expert(w1, rq, D)) * by_expert(w3, rq, D)
    z = by_expert(w2, mxq(h, 0, "e4m3"), D)
    own = np.zeros((N, T))
    own[:, idx] = f64(gate[:1]) * y
    return np.concatenate([own, z], axis=1)

@@ -1,0 +1,208 @@
+from contextlib import ExitStack
+
+import concourse.mybir as mybir
+from concourse.masks import make_identity
+
+K, T, Q, E, C, H, N = 1024, 768, 512, 2, 256, 512, 128
+FLOPS = 2 * (2 * E * C) * (2 * K * H + H * N)
+
+F32 = mybir.dt.float32
+BF16 = mybir.dt.bfloat16
+I32 = mybir.dt.int32
+U32 = mybir.dt.uint32
+U16 = mybir.dt.uint16
+U8 = mybir.dt.uint8
+FP8X4 = mybir.dt.float8_e4m3fn_x4
+MULT = mybir.AluOpType.mult
+SIGMOID = mybir.ActivationFunctionType.Sigmoid
+
+P = 128
+PASSES = K // 512
+LIST_COLS = C // 16
+
+
+def tile_moe_loc_glu_sigmoid_kernel(
+    tc, x_words, x_scales, xo, w1_words, w1_scales, w3_words, w3_scales, w2_words, w2_scales, gate, offs, offs2, out
+):
+    nc = tc.nc
+    with ExitStack() as ctx:
+        keep = ctx.enter_context(tc.tile_pool(name="keep", bufs=1))
+        ring = ctx.enter_context(tc.tile_pool(name="ring", bufs=2))
+        psum = ctx.enter_context(tc.psum_pool(name="psum", bufs=1))
+
+        def held(shape, dtype, name):
+            return keep.tile(shape, dtype, name=name, align_bytes=64)
+
+        own_list = held([P, 2 * LIST_COLS], U16, "own_list")
+        far_list = held([P, 2 * LIST_COLS], U16, "far_list")
+        x_planes = held([P, Q], U8, "x_planes")
+        w1_planes = held([P, H], U8, "w1_planes")
+        w3_planes = held([P, H], U8, "w3_planes")
+        w2_planes = held([P, N], U8, "w2_planes")
+        own_out = held([P, T], F32, "own_out")
+        identity = held([P, P], F32, "identity")
+
+        def load_planes(queue, planes, scales):
+            for q in range(4):
+                rows = scales[:, 4 * q : 4 * q + 4, :]
+                queue.dma_start(planes[32 * q : 32 * q + 4 * scales.shape[0], :].bitcast(I32), rows.bitcast(I32))
+
+        for planes in (x_planes, w1_planes, w3_planes, w2_planes):
+            nc.gpsimd.memset(planes[:].bitcast(I32), 0)
+        nc.vector.memset(own_out[:], 0.0)
+
+        make_identity(nc, identity[:])
+        nc.sync.dma_start(far_list[:], offs2)
+        x_tab = []
+        for s in range(PASSES):
+            tab = held([P, Q], I32, f"x_tab{s}")
+            nc.sync.dma_start(tab[:], x_words[s].rearrange("p t d -> p (t d)").bitcast(I32))
+            x_tab.append(tab)
+        load_planes(nc.sync, x_planes, x_scales)
+
+        def load_first_layer(words, e, name):
+            w = held([P, PASSES, H], I32, name)
+            nc.sync.dma_start(w[:], words[e].rearrange("s p i d -> p s (i d)").bitcast(I32))
+            return w
+
+        def load_own(s, u, pieces=1):
+            rows = xo[512 * s : 512 * (s + 1), :].rearrange("(p u e) t -> p u e t", u=2, e=2)
+            width = T // pieces
+            parts = []
+            for h in range(pieces):
+                raw = held([P, 2, width], F32, f"raw{s}{u}{h}")
+                nc.sync.dma_start(raw[:], rows[:, u, :, width * h : width * (h + 1)])
+                parts.append(raw)
+            return parts
+
+        raws = {(0, 0): load_own(0, 0)}
+        nc.sync.dma_start(own_list[:], offs)
+        raws[0, 1] = load_own(0, 1)
+        raws[1, 0] = load_own(1, 0)
+        w1 = {0: load_first_layer(w1_words, 0, "w1_0")}
+        load_planes(nc.sync, w1_planes, w1_scales.rearrange("e s b i -> (e s) b i"))
+        raws[1, 1] = load_own(1, 1, pieces=2)
+        w3 = {0: load_first_layer(w3_words, 0, "w3_0")}
+        load_planes(nc.sync, w3_planes, w3_scales.rearrange("e s b i -> (e s) b i"))
+        w1[1] = load_first_layer(w1_words, 1, "w1_1")
+        w2 = held([P, E, N], I32, "w2")
+        nc.sync.dma_start(w2[:], w2_words.rearrange("e s p n d -> p (e s) (n d)").bitcast(I32))
+        load_planes(nc.sync, w2_planes, w2_scales.rearrange("e s b n -> (e s) b n"))
+        w3[1] = load_first_layer(w3_words, 1, "w3_1")
+        gate_sb = held([P, E * C], F32, "gate_sb")
+        nc.sync.dma_start(gate_sb[:], gate)
+
+        def expert_list(tile, e):
+            return tile[:, LIST_COLS * e : LIST_COLS * (e + 1)]
+
+        def gather_far(e):
+            codes = []
+            for s in range(PASSES):
+                g = held([P, C], U32, f"far_codes{e}{s}")
+                nc.vector.tensor_copy(g[:], x_tab[s][:].bitcast(U32).indirect(expert_list(far_list, e)))
+                codes.append(g)
+            planes = held([P, C], U8, f"far_planes{e}")
+            nc.vector.tensor_copy(planes[:], x_planes[:].indirect(expert_list(far_list, e)))
+            return [(codes[s], planes, 4 * s) for s in range(PASSES)]
+
+        def cast_pairs(s, u):
+            pairs = held([P, T, 2], BF16, f"pairs{s}{u}")
+            for h, raw in enumerate(raws[s, u]):
+                width = raw.shape[2]
+                nc.scalar.copy(pairs[:, width * h : width * (h + 1), :], raw[:].rearrange("p e t -> p t e"))
+            return pairs[:].rearrange("p t e -> p (t e)").bitcast(U32)
+
+        def gather_own(table, picked, u, offsets):
+            nc.vector.tensor_copy(picked[:, u, :], table.indirect(offsets))
+
+        def quantise_own(picked, width, name):
+            woven = held([P, width, 2], I32, "woven" + name)
+            nc.vector.tensor_copy(woven[:], picked[:].bitcast(I32).rearrange("p u c -> p c u"))
+            codes = held([P, width], U32, "own_codes" + name)
+            planes = held([P, width], U8, "own_planes" + name)
+            nc.vector.quantize_mx(codes[:].bitcast(FP8X4), planes[:], woven[:].rearrange("p c u -> p (c u)").bitcast(BF16))
+            return codes, planes
+
+        def hidden(e, tokens, first):
+            sums = []
+            for w, planes, tag in ((w1[e], w1_planes, "a"), (w3[e], w3_planes, "b")):
+                acc = psum.tile([P, H], F32, name="acc_" + tag, tag="acc_" + tag, bufs=3)
+                for s in range(PASSES):
+                    codes, tok_planes, row, col = tokens[s]
+                    cols = slice(col + first, col + first + P)
+                    nc.tensor.matmul_mx(
+                        out=acc[:],
+                        lhsT=codes[:, cols].bitcast(FP8X4),
+                        lhsT_scale=tok_planes[row:P, cols],
+                        rhs=w[:, s, :].bitcast(FP8X4),
+                        rhs_scale=planes[4 * (PASSES * e + s) : P, :],
+                        start=(s == 0),
+                        stop=(s == PASSES - 1),
+                    )
+                sums.append(acc[:].rearrange("q (p u e) -> q u p e", u=2, e=2))
+            sig = ring.tile([P, 2, P, 2], F32, name="sig", bufs=4)
+            nc.scalar.activation(sig[:], sums[0], SIGMOID)
+            h = ring.tile([P, 2, P, 2], BF16, name="h", bufs=4)
+            nc.vector.tensor_tensor(h[:], sums[1], sig[:], MULT)
+            return h[:].rearrange("q u p e -> q (u p e)").bitcast(F32)
+
+        def second_layer(e, h_words, result):
+            width = P * len(h_words)
+            turned = psum.tile([P, 2, width], F32, name="turned")
+            for j, words in enumerate(h_words):
+                for u in range(2):
+                    nc.tensor.transpose(turned[:, u, P * j : P * (j + 1)], words[:, P * u : P * (u + 1)], identity[:])
+            h_in = ring.tile([P, width, 2], F32, name="h_in", align_bytes=64)
+            nc.scalar.copy(h_in[:], turned[:].rearrange("p u c -> p c u"))
+            h_codes = ring.tile([P, width], U32, name="h_codes", align_bytes=64)
+            h_planes = ring.tile([P, width], U8, name="h_planes", align_bytes=64)
+            nc.vector.quantize_mx(h_codes[:].bitcast(FP8X4), h_planes[:], h_in[:].rearrange("p c u -> p (c u)").bitcast(BF16))
+            y = psum.tile([P, width], F32, name="y")
+            nc.tensor.matmul_mx(
+                out=y[:],
+                lhsT=w2[:, e, :].bitcast(FP8X4),
+                lhsT_scale=w2_planes[4 * e : P, :],
+                rhs=h_codes[:].bitcast(FP8X4),
+                rhs_scale=h_planes[:],
+                start=True,
+                stop=True,
+            )
+            nc.scalar.copy(result, y[:])
+
+        def expert(e, tokens, name, tiles_at_once):
+            result = held([P, C], F32, name)
+            for first in range(0, C // P, tiles_at_once):
+                h_words = [hidden(e, tokens, P * j) for j in range(first, first + tiles_at_once)]
+                second_layer(e, h_words, result[:, P * first : P * (first + tiles_at_once)])
+            return result
+
+        def far_expert(e, far, tiles_at_once):
+            z = expert(e, [(c, pl, row, 0) for c, pl, row in far], f"z{e}", tiles_at_once)
+            nc.sync.dma_start(out[:, T + C * e : T + C * (e + 1)], z[:])
+
+        def own_expert(e, tokens):
+            y = expert(e, tokens, f"y{e}", 2)
+            nc.vector.tensor_tensor(own_out[:].indirect(expert_list(own_list, e)), y[:], gate_sb[:, C * e : C * (e + 1)], MULT)
+
+        far0 = gather_far(0)
+        tables = {(s, u): cast_pairs(s, u) for s in range(PASSES) for u in range(2)}
+        far1 = gather_far(1)
+
+        picked0 = held([P, 2, E * C], U32, "picked0")
+        for u in range(2):
+            gather_own(tables[0, u], picked0, u, own_list[:])
+        codes0, planes0 = quantise_own(picked0, E * C, "0")
+
+        own = []
+        for e in range(E):
+            picked1 = held([P, 2, C], U32, f"picked1{e}")
+            for u in range(2):
+                gather_own(tables[1, u], picked1, u, expert_list(own_list, e))
+            codes1, planes1 = quantise_own(picked1, C, f"1{e}")
+            own.append([(codes0, planes0, 0, C * e), (codes1, planes1, 0, 0)])
+
+        far_expert(0, far0, 2)
+        for e in range(E):
+            own_expert(e, own[e])
+        far_expert(1, far1, 1)
+        nc.sync.dma_start(out[:, 0:T], own_out[:])

@@ -17,8 +17,12 @@ MULT = mybir.AluOpType.mult
 SIGMOID = mybir.ActivationFunctionType.Sigmoid
 
 P = 128
-PASSES = K // 512
-LIST_COLS = C // 16
+K_PASS = 512
+PASSES = K // K_PASS
+PER_COLUMN = 16
+W1_BANKS, W3_BANKS = 2, 4
+SIGMOID_TILES = 4
+H_TILES = 2 * E * C // P
 
 
 def tile_moe_loc_glu_sigmoid_kernel(
@@ -33,8 +37,8 @@ def tile_moe_loc_glu_sigmoid_kernel(
         def held(shape, dtype, name):
             return keep.tile(shape, dtype, name=name, align_bytes=64)
 
-        own_list = held([P, 2 * LIST_COLS], U16, "own_list")
-        far_list = held([P, 2 * LIST_COLS], U16, "far_list")
+        own_list = held([P, E * C // PER_COLUMN], U16, "own_list")
+        far_list = held([P, E * C // PER_COLUMN], U16, "far_list")
         x_planes = held([P, Q], U8, "x_planes")
         w1_planes = held([P, H], U8, "w1_planes")
         w3_planes = held([P, H], U8, "w3_planes")
@@ -42,124 +46,130 @@ def tile_moe_loc_glu_sigmoid_kernel(
         own_out = held([P, T], F32, "own_out")
         identity = held([P, P], F32, "identity")
 
+        for planes in (x_planes, w1_planes, w3_planes, w2_planes):
+            nc.gpsimd.memset(planes[:].bitcast(I32), 0)
+        nc.vector.memset(own_out[:], 0.0)
+
+        warm = held([P, 1], F32, "warm")
+        nc.scalar.activation(warm[:], own_out[:, 0:1], SIGMOID)
+
         def load_planes(queue, planes, scales):
             for q in range(4):
                 rows = scales[:, 4 * q : 4 * q + 4, :]
                 queue.dma_start(planes[32 * q : 32 * q + 4 * scales.shape[0], :].bitcast(I32), rows.bitcast(I32))
 
-        for planes in (x_planes, w1_planes, w3_planes, w2_planes):
-            nc.gpsimd.memset(planes[:].bitcast(I32), 0)
-        nc.vector.memset(own_out[:], 0.0)
+        def load_words(source, name):
+            words = held([P, source.shape[1]], I32, name)
+            nc.sync.dma_start(words[:], source.rearrange("p c d -> p (c d)").bitcast(I32))
+            return words
 
-        make_identity(nc, identity[:])
-        nc.sync.dma_start(far_list[:], offs2)
-        x_tab = []
-        for s in range(PASSES):
-            tab = held([P, Q], I32, f"x_tab{s}")
-            nc.sync.dma_start(tab[:], x_words[s].rearrange("p t d -> p (t d)").bitcast(I32))
-            x_tab.append(tab)
-        load_planes(nc.sync, x_planes, x_scales)
-
-        def load_first_layer(words, e, name):
-            w = held([P, PASSES, H], I32, name)
-            nc.sync.dma_start(w[:], words[e].rearrange("s p i d -> p s (i d)").bitcast(I32))
-            return w
-
-        def load_own(s, u, pieces=1):
-            rows = xo[512 * s : 512 * (s + 1), :].rearrange("(p u e) t -> p u e t", u=2, e=2)
+        def load_own(s, u, pieces):
+            rows = xo[K_PASS * s : K_PASS * (s + 1), :].rearrange("(p u e) t -> p u e t", u=2, e=2)
             width = T // pieces
             parts = []
-            for h in range(pieces):
-                raw = held([P, 2, width], F32, f"raw{s}{u}{h}")
-                nc.sync.dma_start(raw[:], rows[:, u, :, width * h : width * (h + 1)])
+            for piece in range(pieces):
+                raw = held([P, 2, width], F32, f"raw{s}{u}{piece}")
+                nc.sync.dma_start(raw[:], rows[:, u, :, width * piece : width * (piece + 1)])
                 parts.append(raw)
             return parts
 
-        raws = {(0, 0): load_own(0, 0)}
+        load_planes(nc.gpsimd, w3_planes, w3_scales.rearrange("e s b i -> (e s) b i"))
+        make_identity(nc, identity[:])
+
+        raws, w1, w3, x_table = {}, {}, {}, {}
+        nc.sync.dma_start(far_list[:], offs2)
+        x_table[0] = load_words(x_words[0], "x_table0")
+        raws[0, 0] = load_own(0, 0, 1)
+        x_table[1] = load_words(x_words[1], "x_table1")
         nc.sync.dma_start(own_list[:], offs)
-        raws[0, 1] = load_own(0, 1)
-        raws[1, 0] = load_own(1, 0)
-        w1 = {0: load_first_layer(w1_words, 0, "w1_0")}
+        load_planes(nc.sync, x_planes, x_scales)
+        raws[0, 1] = load_own(0, 1, 2)
+        raws[1, 0] = load_own(1, 0, 2)
         load_planes(nc.sync, w1_planes, w1_scales.rearrange("e s b i -> (e s) b i"))
-        raws[1, 1] = load_own(1, 1, pieces=2)
-        w3 = {0: load_first_layer(w3_words, 0, "w3_0")}
-        load_planes(nc.sync, w3_planes, w3_scales.rearrange("e s b i -> (e s) b i"))
-        w1[1] = load_first_layer(w1_words, 1, "w1_1")
+        w1[0, 0] = load_words(w1_words[0, 0], "w1_00")
+        raws[1, 1] = load_own(1, 1, 2)
+        w3[0, 0] = load_words(w3_words[0, 0], "w3_00")
+        for e, s in ((0, 1), (1, 0), (1, 1)):
+            w1[e, s] = load_words(w1_words[e, s], f"w1_{e}{s}")
+            w3[e, s] = load_words(w3_words[e, s], f"w3_{e}{s}")
         w2 = held([P, E, N], I32, "w2")
         nc.sync.dma_start(w2[:], w2_words.rearrange("e s p n d -> p (e s) (n d)").bitcast(I32))
         load_planes(nc.sync, w2_planes, w2_scales.rearrange("e s b n -> (e s) b n"))
-        w3[1] = load_first_layer(w3_words, 1, "w3_1")
         gate_sb = held([P, E * C], F32, "gate_sb")
         nc.sync.dma_start(gate_sb[:], gate)
 
-        def expert_list(tile, e):
-            return tile[:, LIST_COLS * e : LIST_COLS * (e + 1)]
+        def entries(a_list, first, count):
+            return a_list[:, first // PER_COLUMN : (first + count) // PER_COLUMN]
 
         def gather_far(e):
+            offsets = entries(far_list, C * e, C)
             codes = []
             for s in range(PASSES):
-                g = held([P, C], U32, f"far_codes{e}{s}")
-                nc.vector.tensor_copy(g[:], x_tab[s][:].bitcast(U32).indirect(expert_list(far_list, e)))
-                codes.append(g)
+                picked = held([P, C], U32, f"far_codes{e}{s}")
+                nc.vector.tensor_copy(picked[:], x_table[s][:].bitcast(U32).indirect(offsets))
+                codes.append(picked)
             planes = held([P, C], U8, f"far_planes{e}")
-            nc.vector.tensor_copy(planes[:], x_planes[:].indirect(expert_list(far_list, e)))
-            return [(codes[s], planes, 4 * s) for s in range(PASSES)]
+            nc.vector.tensor_copy(planes[:], x_planes[:].indirect(offsets))
+            return [(codes[s], planes, 4 * s, 0) for s in range(PASSES)]
 
         def cast_pairs(s, u):
             pairs = held([P, T, 2], BF16, f"pairs{s}{u}")
-            for h, raw in enumerate(raws[s, u]):
+            for piece, raw in enumerate(raws[s, u]):
                 width = raw.shape[2]
-                nc.scalar.copy(pairs[:, width * h : width * (h + 1), :], raw[:].rearrange("p e t -> p t e"))
+                nc.scalar.copy(pairs[:, width * piece : width * (piece + 1), :], raw[:].rearrange("p e t -> p t e"))
             return pairs[:].rearrange("p t e -> p (t e)").bitcast(U32)
 
-        def gather_own(table, picked, u, offsets):
-            nc.vector.tensor_copy(picked[:, u, :], table.indirect(offsets))
-
-        def quantise_own(picked, width, name):
-            woven = held([P, width, 2], I32, "woven" + name)
-            nc.vector.tensor_copy(woven[:], picked[:].bitcast(I32).rearrange("p u c -> p c u"))
-            codes = held([P, width], U32, "own_codes" + name)
-            planes = held([P, width], U8, "own_planes" + name)
+        def own_operand(s, first, count, weave_on_scalar):
+            picked = held([P, 2, count], U32, f"picked{s}_{first}")
+            for u in range(2):
+                nc.vector.tensor_copy(picked[:, u, :], tables[s, u].indirect(entries(own_list, first, count)))
+            woven = held([P, count, 2], I32, f"woven{s}_{first}")
+            if weave_on_scalar:
+                nc.scalar.copy(woven[:].bitcast(U32), picked[:].rearrange("p u c -> p c u"))
+            else:
+                nc.vector.tensor_copy(woven[:], picked[:].bitcast(I32).rearrange("p u c -> p c u"))
+            codes = held([P, count], U32, f"own_codes{s}_{first}")
+            planes = held([P, count], U8, f"own_planes{s}_{first}")
             nc.vector.quantize_mx(codes[:].bitcast(FP8X4), planes[:], woven[:].rearrange("p c u -> p (c u)").bitcast(BF16))
             return codes, planes
 
-        def hidden(e, tokens, first):
+        def hidden(e, tokens, j):
             sums = []
-            for w, planes, tag in ((w1[e], w1_planes, "a"), (w3[e], w3_planes, "b")):
-                acc = psum.tile([P, H], F32, name="acc_" + tag, tag="acc_" + tag, bufs=3)
+            for w, w_planes, tag, banks in ((w1, w1_planes, "a", W1_BANKS), (w3, w3_planes, "b", W3_BANKS)):
+                acc = psum.tile([P, H], F32, name="acc_" + tag, tag="acc_" + tag, bufs=banks)
                 for s in range(PASSES):
-                    codes, tok_planes, row, col = tokens[s]
-                    cols = slice(col + first, col + first + P)
+                    codes, planes, first, column = tokens[s]
+                    slots = slice(column + P * j, column + P * (j + 1))
                     nc.tensor.matmul_mx(
                         out=acc[:],
-                        lhsT=codes[:, cols].bitcast(FP8X4),
-                        lhsT_scale=tok_planes[row:P, cols],
-                        rhs=w[:, s, :].bitcast(FP8X4),
-                        rhs_scale=planes[4 * (PASSES * e + s) : P, :],
+                        lhsT=codes[:, slots].bitcast(FP8X4),
+                        lhsT_scale=planes[first:P, slots],
+                        rhs=w[e, s][:].bitcast(FP8X4),
+                        rhs_scale=w_planes[4 * (PASSES * e + s) : P, :],
                         start=(s == 0),
                         stop=(s == PASSES - 1),
                     )
                 sums.append(acc[:].rearrange("q (p u e) -> q u p e", u=2, e=2))
-            sig = ring.tile([P, 2, P, 2], F32, name="sig", bufs=4)
+            sig = ring.tile([P, 2, P, 2], F32, name="sig", bufs=SIGMOID_TILES)
             nc.scalar.activation(sig[:], sums[0], SIGMOID)
-            h = ring.tile([P, 2, P, 2], BF16, name="h", bufs=4)
+            h = ring.tile([P, 2, P, 2], BF16, name="h", bufs=H_TILES)
             nc.vector.tensor_tensor(h[:], sums[1], sig[:], MULT)
             return h[:].rearrange("q u p e -> q (u p e)").bitcast(F32)
 
-        def second_layer(e, h_words, result):
-            width = P * len(h_words)
+        def second_layer(e, h_tiles, result):
+            width = P * len(h_tiles)
             turned = psum.tile([P, 2, width], F32, name="turned")
-            for j, words in enumerate(h_words):
+            for j, h_pairs in enumerate(h_tiles):
                 for u in range(2):
-                    nc.tensor.transpose(turned[:, u, P * j : P * (j + 1)], words[:, P * u : P * (u + 1)], identity[:])
-            h_in = ring.tile([P, width, 2], F32, name="h_in", align_bytes=64)
-            nc.scalar.copy(h_in[:], turned[:].rearrange("p u c -> p c u"))
+                    nc.tensor.transpose(turned[:, u, P * j : P * (j + 1)], h_pairs[:, P * u : P * (u + 1)], identity[:])
+            h_woven = ring.tile([P, width, 2], F32, name="h_woven", align_bytes=64)
+            nc.scalar.copy(h_woven[:], turned[:].rearrange("p u c -> p c u"))
             h_codes = ring.tile([P, width], U32, name="h_codes", align_bytes=64)
             h_planes = ring.tile([P, width], U8, name="h_planes", align_bytes=64)
-            nc.vector.quantize_mx(h_codes[:].bitcast(FP8X4), h_planes[:], h_in[:].rearrange("p c u -> p (c u)").bitcast(BF16))
-            y = psum.tile([P, width], F32, name="y")
+            nc.vector.quantize_mx(h_codes[:].bitcast(FP8X4), h_planes[:], h_woven[:].rearrange("p c u -> p (c u)").bitcast(BF16))
+            product = psum.tile([P, width], F32, name="product")
             nc.tensor.matmul_mx(
-                out=y[:],
+                out=product[:],
                 lhsT=w2[:, e, :].bitcast(FP8X4),
                 lhsT_scale=w2_planes[4 * e : P, :],
                 rhs=h_codes[:].bitcast(FP8X4),
@@ -167,42 +177,41 @@ def tile_moe_loc_glu_sigmoid_kernel(
                 start=True,
                 stop=True,
             )
-            nc.scalar.copy(result, y[:])
+            nc.scalar.copy(result, product[:])
 
-        def expert(e, tokens, name, tiles_at_once):
-            result = held([P, C], F32, name)
-            for first in range(0, C // P, tiles_at_once):
-                h_words = [hidden(e, tokens, P * j) for j in range(first, first + tiles_at_once)]
-                second_layer(e, h_words, result[:, P * first : P * (first + tiles_at_once)])
-            return result
+        z = [held([P, C], F32, f"z{e}") for e in range(E)]
+        y = [held([P, C], F32, f"y{e}") for e in range(E)]
 
-        def far_expert(e, far, tiles_at_once):
-            z = expert(e, [(c, pl, row, 0) for c, pl, row in far], f"z{e}", tiles_at_once)
-            nc.sync.dma_start(out[:, T + C * e : T + C * (e + 1)], z[:])
+        def store_far(e):
+            nc.sync.dma_start(out[:, T + C * e : T + C * (e + 1)], z[e][:])
 
-        def own_expert(e, tokens):
-            y = expert(e, tokens, f"y{e}", 2)
-            nc.vector.tensor_tensor(own_out[:].indirect(expert_list(own_list, e)), y[:], gate_sb[:, C * e : C * (e + 1)], MULT)
+        def scatter(e, first, count):
+            slot = C * e + first
+            window = own_out[:].indirect(entries(own_list, slot, count))
+            nc.vector.tensor_tensor(window, y[e][:, first : first + count], gate_sb[:, slot : slot + count], MULT)
 
-        far0 = gather_far(0)
+        far = [gather_far(e) for e in range(E)]
         tables = {(s, u): cast_pairs(s, u) for s in range(PASSES) for u in range(2)}
-        far1 = gather_far(1)
 
-        picked0 = held([P, 2, E * C], U32, "picked0")
-        for u in range(2):
-            gather_own(tables[0, u], picked0, u, own_list[:])
-        codes0, planes0 = quantise_own(picked0, E * C, "0")
-
+        codes0, planes0 = own_operand(0, 0, E * C, False)
         own = []
         for e in range(E):
-            picked1 = held([P, 2, C], U32, f"picked1{e}")
-            for u in range(2):
-                gather_own(tables[1, u], picked1, u, expert_list(own_list, e))
-            codes1, planes1 = quantise_own(picked1, C, f"1{e}")
+            codes1, planes1 = own_operand(1, C * e, C, True)
             own.append([(codes0, planes0, 0, C * e), (codes1, planes1, 0, 0)])
 
-        far_expert(0, far0, 2)
-        for e in range(E):
-            own_expert(e, own[e])
-        far_expert(1, far1, 1)
+        h_far0 = [hidden(0, far[0], j) for j in range(2)]
+        h_own0 = [hidden(0, own[0], j) for j in range(2)]
+        h_own1 = [hidden(1, own[1], 0)]
+        second_layer(0, h_far0, z[0][:])
+        store_far(0)
+        h_own1.append(hidden(1, own[1], 1))
+        second_layer(0, h_own0, y[0][:])
+        scatter(0, 0, C)
+        for j in range(2):
+            second_layer(1, [h_own1[j]], y[1][:, P * j : P * (j + 1)])
+        scatter(1, 0, P)
+        h_far1 = [hidden(1, far[1], j) for j in range(2)]
+        scatter(1, P, P)
+        second_layer(1, h_far1, z[1][:])
+        store_far(1)
         nc.sync.dma_start(out[:, 0:T], own_out[:])

@@ -179,16 +179,18 @@ def tile_moe_loc_glu_sigmoid_kernel(
             )
             nc.scalar.copy(result, product[:])
 
-        z = [held([P, C], F32, f"z{e}") for e in range(E)]
-        y = [held([P, C], F32, f"y{e}") for e in range(E)]
+        def far_expert(e):
+            z = held([P, C], F32, f"z{e}")
+            second_layer(e, [hidden(e, far[e], j) for j in range(C // P)], z[:])
+            nc.sync.dma_start(out[:, T + C * e : T + C * (e + 1)], z[:])
 
-        def store_far(e):
-            nc.sync.dma_start(out[:, T + C * e : T + C * (e + 1)], z[e][:])
-
-        def scatter(e, first, count):
-            slot = C * e + first
-            window = own_out[:].indirect(entries(own_list, slot, count))
-            nc.vector.tensor_tensor(window, y[e][:, first : first + count], gate_sb[:, slot : slot + count], MULT)
+        def own_expert(e):
+            for j in range(C // P):
+                slot = C * e + P * j
+                y = held([P, P], F32, f"y{e}{j}")
+                second_layer(e, [hidden(e, own[e], j)], y[:])
+                window = own_out[:].indirect(entries(own_list, slot, P))
+                nc.vector.tensor_tensor(window, y[:], gate_sb[:, slot : slot + P], MULT)
 
         far = [gather_far(e) for e in range(E)]
         tables = {(s, u): cast_pairs(s, u) for s in range(PASSES) for u in range(2)}
@@ -199,19 +201,8 @@ def tile_moe_loc_glu_sigmoid_kernel(
             codes1, planes1 = own_operand(1, C * e, C, True)
             own.append([(codes0, planes0, 0, C * e), (codes1, planes1, 0, 0)])
 
-        h_far0 = [hidden(0, far[0], j) for j in range(2)]
-        h_own0 = [hidden(0, own[0], j) for j in range(2)]
-        h_own1 = [hidden(1, own[1], 0)]
-        second_layer(0, h_far0, z[0][:])
-        store_far(0)
-        h_own1.append(hidden(1, own[1], 1))
-        second_layer(0, h_own0, y[0][:])
-        scatter(0, 0, C)
-        for j in range(2):
-            second_layer(1, [h_own1[j]], y[1][:, P * j : P * (j + 1)])
-        scatter(1, 0, P)
-        h_far1 = [hidden(1, far[1], j) for j in range(2)]
-        scatter(1, P, P)
-        second_layer(1, h_far1, z[1][:])
-        store_far(1)
+        far_expert(0)
+        for e in range(E):
+            own_expert(e)
+        far_expert(1)
         nc.sync.dma_start(out[:, 0:T], own_out[:])

from contextlib import ExitStack

import concourse.mybir as mybir
from concourse.masks import make_identity

K, T, Q, E, C, H, N = 1024, 768, 512, 2, 256, 512, 128
FLOPS = 2 * (2 * E * C) * (2 * K * H + H * N)

F32 = mybir.dt.float32
BF16 = mybir.dt.bfloat16
I32 = mybir.dt.int32
U32 = mybir.dt.uint32
U16 = mybir.dt.uint16
U8 = mybir.dt.uint8
FP8X4 = mybir.dt.float8_e4m3fn_x4
MULT = mybir.AluOpType.mult
SIGMOID = mybir.ActivationFunctionType.Sigmoid

P = 128
K_PASS = 512
PASSES = K // K_PASS
PER_COLUMN = 16
W1_BANKS, W3_BANKS = 2, 4
SIGMOID_TILES = 4
H_TILES = 2 * E * C // P


def tile_moe_loc_glu_sigmoid_kernel(
    tc, x_words, x_scales, xo, w1_words, w1_scales, w3_words, w3_scales, w2_words, w2_scales, gate, offs, offs2, out
):
    nc = tc.nc
    with ExitStack() as ctx:
        keep = ctx.enter_context(tc.tile_pool(name="keep", bufs=1))
        ring = ctx.enter_context(tc.tile_pool(name="ring", bufs=2))
        psum = ctx.enter_context(tc.psum_pool(name="psum", bufs=1))

        def held(shape, dtype, name):
            return keep.tile(shape, dtype, name=name, align_bytes=64)

        own_list = held([P, E * C // PER_COLUMN], U16, "own_list")
        far_list = held([P, E * C // PER_COLUMN], U16, "far_list")
        x_planes = held([P, Q], U8, "x_planes")
        w1_planes = held([P, H], U8, "w1_planes")
        w3_planes = held([P, H], U8, "w3_planes")
        w2_planes = held([P, N], U8, "w2_planes")
        own_out = held([P, T], F32, "own_out")
        identity = held([P, P], F32, "identity")

        for planes in (x_planes, w1_planes, w3_planes, w2_planes):
            nc.gpsimd.memset(planes[:].bitcast(I32), 0)
        nc.vector.memset(own_out[:], 0.0)

        warm = held([P, 1], F32, "warm")
        nc.scalar.activation(warm[:], own_out[:, 0:1], SIGMOID)

        def load_planes(queue, planes, scales):
            for q in range(4):
                rows = scales[:, 4 * q : 4 * q + 4, :]
                queue.dma_start(planes[32 * q : 32 * q + 4 * scales.shape[0], :].bitcast(I32), rows.bitcast(I32))

        def load_words(source, name):
            words = held([P, source.shape[1]], I32, name)
            nc.sync.dma_start(words[:], source.rearrange("p c d -> p (c d)").bitcast(I32))
            return words

        def load_own(s, u, pieces):
            rows = xo[K_PASS * s : K_PASS * (s + 1), :].rearrange("(p u e) t -> p u e t", u=2, e=2)
            width = T // pieces
            parts = []
            for piece in range(pieces):
                raw = held([P, 2, width], F32, f"raw{s}{u}{piece}")
                nc.sync.dma_start(raw[:], rows[:, u, :, width * piece : width * (piece + 1)])
                parts.append(raw)
            return parts

        load_planes(nc.gpsimd, w3_planes, w3_scales.rearrange("e s b i -> (e s) b i"))
        make_identity(nc, identity[:])

        raws, w1, w3, x_table = {}, {}, {}, {}
        nc.sync.dma_start(far_list[:], offs2)
        x_table[0] = load_words(x_words[0], "x_table0")
        raws[0, 0] = load_own(0, 0, 1)
        x_table[1] = load_words(x_words[1], "x_table1")
        nc.sync.dma_start(own_list[:], offs)
        load_planes(nc.sync, x_planes, x_scales)
        raws[0, 1] = load_own(0, 1, 2)
        raws[1, 0] = load_own(1, 0, 2)
        load_planes(nc.sync, w1_planes, w1_scales.rearrange("e s b i -> (e s) b i"))
        w1[0, 0] = load_words(w1_words[0, 0], "w1_00")
        raws[1, 1] = load_own(1, 1, 2)
        w3[0, 0] = load_words(w3_words[0, 0], "w3_00")
        for e, s in ((0, 1), (1, 0), (1, 1)):
            w1[e, s] = load_words(w1_words[e, s], f"w1_{e}{s}")
            w3[e, s] = load_words(w3_words[e, s], f"w3_{e}{s}")
        w2 = held([P, E, N], I32, "w2")
        nc.sync.dma_start(w2[:], w2_words.rearrange("e s p n d -> p (e s) (n d)").bitcast(I32))
        load_planes(nc.sync, w2_planes, w2_scales.rearrange("e s b n -> (e s) b n"))
        gate_sb = held([P, E * C], F32, "gate_sb")
        nc.sync.dma_start(gate_sb[:], gate)

        def entries(a_list, first, count):
            return a_list[:, first // PER_COLUMN : (first + count) // PER_COLUMN]

        def gather_far(e):
            offsets = entries(far_list, C * e, C)
            codes = []
            for s in range(PASSES):
                picked = held([P, C], U32, f"far_codes{e}{s}")
                nc.vector.tensor_copy(picked[:], x_table[s][:].bitcast(U32).indirect(offsets))
                codes.append(picked)
            planes = held([P, C], U8, f"far_planes{e}")
            nc.vector.tensor_copy(planes[:], x_planes[:].indirect(offsets))
            return [(codes[s], planes, 4 * s, 0) for s in range(PASSES)]

        def cast_pairs(s, u):
            pairs = held([P, T, 2], BF16, f"pairs{s}{u}")
            for piece, raw in enumerate(raws[s, u]):
                width = raw.shape[2]
                nc.scalar.copy(pairs[:, width * piece : width * (piece + 1), :], raw[:].rearrange("p e t -> p t e"))
            return pairs[:].rearrange("p t e -> p (t e)").bitcast(U32)

        def own_operand(s, first, count, weave_on_scalar):
            picked = held([P, 2, count], U32, f"picked{s}_{first}")
            for u in range(2):
                nc.vector.tensor_copy(picked[:, u, :], tables[s, u].indirect(entries(own_list, first, count)))
            woven = held([P, count, 2], I32, f"woven{s}_{first}")
            if weave_on_scalar:
                nc.scalar.copy(woven[:].bitcast(U32), picked[:].rearrange("p u c -> p c u"))
            else:
                nc.vector.tensor_copy(woven[:], picked[:].bitcast(I32).rearrange("p u c -> p c u"))
            codes = held([P, count], U32, f"own_codes{s}_{first}")
            planes = held([P, count], U8, f"own_planes{s}_{first}")
            nc.vector.quantize_mx(codes[:].bitcast(FP8X4), planes[:], woven[:].rearrange("p c u -> p (c u)").bitcast(BF16))
            return codes, planes

        def hidden(e, tokens, j):
            sums = []
            for w, w_planes, tag, banks in ((w1, w1_planes, "a", W1_BANKS), (w3, w3_planes, "b", W3_BANKS)):
                acc = psum.tile([P, H], F32, name="acc_" + tag, tag="acc_" + tag, bufs=banks)
                for s in range(PASSES):
                    codes, planes, first, column = tokens[s]
                    slots = slice(column + P * j, column + P * (j + 1))
                    nc.tensor.matmul_mx(
                        out=acc[:],
                        lhsT=codes[:, slots].bitcast(FP8X4),
                        lhsT_scale=planes[first:P, slots],
                        rhs=w[e, s][:].bitcast(FP8X4),
                        rhs_scale=w_planes[4 * (PASSES * e + s) : P, :],
                        start=(s == 0),
                        stop=(s == PASSES - 1),
                    )
                sums.append(acc[:].rearrange("q (p u e) -> q u p e", u=2, e=2))
            sig = ring.tile([P, 2, P, 2], F32, name="sig", bufs=SIGMOID_TILES)
            nc.scalar.activation(sig[:], sums[0], SIGMOID)
            h = ring.tile([P, 2, P, 2], BF16, name="h", bufs=H_TILES)
            nc.vector.tensor_tensor(h[:], sums[1], sig[:], MULT)
            return h[:].rearrange("q u p e -> q (u p e)").bitcast(F32)

        def second_layer(e, h_tiles, result):
            width = P * len(h_tiles)
            turned = psum.tile([P, 2, width], F32, name="turned")
            for j, h_pairs in enumerate(h_tiles):
                for u in range(2):
                    nc.tensor.transpose(turned[:, u, P * j : P * (j + 1)], h_pairs[:, P * u : P * (u + 1)], identity[:])
            h_woven = ring.tile([P, width, 2], F32, name="h_woven", align_bytes=64)
            nc.scalar.copy(h_woven[:], turned[:].rearrange("p u c -> p c u"))
            h_codes = ring.tile([P, width], U32, name="h_codes", align_bytes=64)
            h_planes = ring.tile([P, width], U8, name="h_planes", align_bytes=64)
            nc.vector.quantize_mx(h_codes[:].bitcast(FP8X4), h_planes[:], h_woven[:].rearrange("p c u -> p (c u)").bitcast(BF16))
            product = psum.tile([P, width], F32, name="product")
            nc.tensor.matmul_mx(
                out=product[:],
                lhsT=w2[:, e, :].bitcast(FP8X4),
                lhsT_scale=w2_planes[4 * e : P, :],
                rhs=h_codes[:].bitcast(FP8X4),
                rhs_scale=h_planes[:],
                start=True,
                stop=True,
            )
            nc.scalar.copy(result, product[:])

        def far_expert(e):
            z = held([P, C], F32, f"z{e}")
            second_layer(e, [hidden(e, far[e], j) for j in range(C // P)], z[:])
            nc.sync.dma_start(out[:, T + C * e : T + C * (e + 1)], z[:])

        def own_expert(e):
            for j in range(C // P):
                slot = C * e + P * j
                y = held([P, P], F32, f"y{e}{j}")
                second_layer(e, [hidden(e, own[e], j)], y[:])
                window = own_out[:].indirect(entries(own_list, slot, P))
                nc.vector.tensor_tensor(window, y[:], gate_sb[:, slot : slot + P], MULT)

        far = [gather_far(e) for e in range(E)]
        tables = {(s, u): cast_pairs(s, u) for s in range(PASSES) for u in range(2)}

        codes0, planes0 = own_operand(0, 0, E * C, False)
        own = []
        for e in range(E):
            codes1, planes1 = own_operand(1, C * e, C, True)
            own.append([(codes0, planes0, 0, C * e), (codes1, planes1, 0, 0)])

        far_expert(0)
        for e in range(E):
            own_expert(e)
        far_expert(1)
        nc.sync.dma_start(out[:, 0:T], own_out[:])
